import numpy as np
import ml_dtypes


def mxq(x, axis, fmt="e4m3"):
    dtype, down = {"e4m3": (ml_dtypes.float8_e4m3fn, 7), "e5m2": (ml_dtypes.float8_e5m2, 14)}[fmt]
    v = np.moveaxis(np.asarray(x, np.float32).astype(ml_dtypes.bfloat16).astype(np.float64), axis, -1)
    blocks = v.reshape(v.shape[:-1] + (-1, 32))
    amax = np.abs(blocks).max(-1, keepdims=True)
    byte = np.maximum(np.where(amax > 0, np.frexp(amax)[1] - 1 + 127, 0) - down, 1)
    scale = np.exp2(byte - 127.0)
    codes = (blocks / scale).astype(np.float32).astype(dtype).astype(np.float64)
    return np.moveaxis((codes * scale).reshape(v.shape), -1, axis)


WIDE = False


def mx_kscale(k):
    if not WIDE:
        return np.ones(k)
    levels = np.array([10, -10, 5, -5, 0])
    if k % 512:
        return np.exp2(np.random.permutation(np.resize(levels, k // 32))).repeat(32)
    a = np.empty((k // 512, 16))
    for p in range(k // 512):
        a[p, :8] = np.random.permutation(np.resize(levels, 8))
        for g in range(8):
            far = levels[np.abs(levels - a[p, g]) >= 10]
            a[p, g + 8] = far[np.random.randint(len(far))]
    return np.exp2(a.ravel()).repeat(32)


def f64(x):
    return np.asarray(x).astype(np.float64)


def striped(idx):
    return np.tile(idx.reshape(-1, 16).T, (8, 1)).astype(np.uint16)


def unstriped(offs):
    return offs[:16].T.reshape(-1).astype(np.int64)


E2M1 = np.array([0.0, 0.5, 1.0, 1.5, 2.0, 3.0, 4.0, 6.0, -0.0, -0.5, -1.0, -1.5, -2.0, -3.0, -4.0, -6.0])


def pack_weight(w, fmt):
    k, n = w.shape
    w = f64(np.asarray(w, np.float32).astype(ml_dtypes.bfloat16)).reshape(k // 32, 32, n)
    amax = np.abs(w).max(1)
    if fmt == "e4m3":
        byte = np.frexp(amax)[1] - 1 + 127 - 7
    else:
        mant, ex = np.frexp(amax / 6.0)
        byte = np.where(mant > 0.5, ex, ex - 1) + 127
    byte = np.clip(np.where(amax > 0, byte, 1), 1, 254)
    scaled = (w * np.exp2(127.0 - byte)[:, None, :]).reshape(k, n).astype(np.float32)
    by_word = np.ascontiguousarray(scaled.reshape(k // 512, 128, 4, n).transpose(0, 1, 3, 2))
    if fmt == "e4m3":
        words = by_word.astype(ml_dtypes.float8_e4m3fn).view(np.uint8)
    else:
        c = by_word.astype(ml_dtypes.float4_e2m1fn).view(np.uint8) & 0xF
        words = (c[..., 0::2] | (c[..., 1::2] << 4)).reshape(k // 512, 128, 2 * n)
    return np.ascontiguousarray(words), np.ascontiguousarray(byte.astype(np.uint8).reshape(k // 512, 16, n))


def unpack_weight(words, scales, fmt):
    g, _, n = scales.shape
    words = np.ascontiguousarray(words).reshape(g, 128, n, -1)
    if fmt == "e4m3":
        vals = words.view(ml_dtypes.float8_e4m3fn).astype(np.float64)
    else:
        nib = np.empty((g, 128, n, 4), np.uint8)
        nib[..., 0::2] = words & 0xF
        nib[..., 1::2] = words >> 4
        vals = E2M1[nib]
    vals = vals * np.repeat(np.exp2(scales.astype(np.float64) - 127.0), 8, axis=1)[..., None]
    return vals.transpose(0, 1, 3, 2).reshape(g * 512, n)


def gelu(v):
    return 0.5 * v * (1.0 + np.tanh(np.sqrt(2.0 / np.pi) * (v + 0.044715 * v**3)))


K, KA, KB, H, T, S, T3, S2, T2, P = 1024, 512, 512, 1024, 4096, 1024, 2048, 1024, 2048, 512

def setup_inputs():
    n = np.random.standard_normal
    s = mx_kscale(K)[:, None]
    u = mx_kscale(H)[:, None]
    tab_words, tab_scales = pack_weight(n((K, T)) * s, "e4m3")
    tab2_words, tab2_scales = pack_weight(n((H, T3)) / np.sqrt(H) / u, "e4m3")
    w4_words, w4_scales = pack_weight(n((KA, H)) / np.sqrt(K) / s[:KA], "e2m1")
    return {
        "tab_words": tab_words, "tab_scales": tab_scales,
        "tab2_words": tab2_words, "tab2_scales": tab2_scales,
        "w4_words": w4_words, "w4_scales": w4_scales,
        "w1": (n((KB, H)) / np.sqrt(K) / s[KA:]).astype(np.float32),
        "gain": (np.exp(0.4 * n(H)) * u[:, 0]).astype(np.float32),
        "page0": (n((H, T2)) * u).astype(np.float32),
        "wgs": np.exp(0.3 * n((128, S))).astype(np.float32),
        "season": (1.2 * n(H)).astype(np.float32),
        "cand": (0.6 * n(S2)).astype(np.float32),
        "offs": striped(np.random.permutation(T)[:S]),
        "offs2": striped(np.random.permutation(T3)[:S2]),
        "offs3": striped(np.random.permutation(T2)[:S]),
        "offs4": striped(np.random.permutation(T2)[:P]),
    }

def reference(tab_words, tab_scales, tab2_words, tab2_scales, w4_words, w4_scales, w1, gain, page0, wgs, season, cand, offs, offs2, offs3, offs4):
    v = unpack_weight(tab_words, tab_scales, "e4m3")[:, unstriped(offs)]
    v2 = unpack_weight(tab2_words, tab2_scales, "e4m3")[:, unstriped(offs2)]
    w4 = unpack_weight(w4_words, w4_scales, "e2m1")
    w1q = mxq(f64(w1), 0, "e4m3")
    h = f64(gain)[:, None] * (w4.T @ v[:KA] + w1q.T @ v[KA:])
    page = f64(page0).copy()
    page[:, unstriped(offs3)] = np.tile(f64(wgs), (H // 128, 1)) * h
    x = page[:, unstriped(offs4)]
    xa = mxq(np.abs(x), 0, "e4m3")
    xb = mxq(f64(season)[:, None] * x, 0, "e4m3")
    ea = v2.T @ xa
    eb = v2.T @ xb
    return ea * np.tanh(eb) + f64(cand)[:, None]

@@ -1,0 +1,284 @@
+from contextlib import ExitStack
+
+import concourse.mybir as mybir
+
+K, H, T, S, T3, S2, T2, NB = 1024, 1024, 4096, 1024, 2048, 1024, 2048, 512
+FLOPS = 2 * K * H * S + 2 * 2 * H * S2 * NB
+
+F32 = mybir.dt.float32
+BF16 = mybir.dt.bfloat16
+I32 = mybir.dt.int32
+U32 = mybir.dt.uint32
+U16 = mybir.dt.uint16
+U8 = mybir.dt.uint8
+FP8X4 = mybir.dt.float8_e4m3fn_x4
+FP4X4 = mybir.dt.float4_e2m1fn_x4
+ALU = mybir.AluOpType
+ACT = mybir.ActivationFunctionType
+
+P = 128
+PACK = 4
+BANK = 512
+ALIGN = 64
+SLICES = H // P
+M_TILES = S2 // P
+HALF_TILES = M_TILES // 2
+TAB_PLANE_ROW = (0, 4)
+TAB2_PLANE_ROW = (8, 12)
+
+
+def tile_list_seed_shop_candidates_kernel(
+    tc, tab_words, tab_scales, tab2_words, tab2_scales, w4_words, w4_scales, w1, gain, page0, wgs,
+    season, cand, offs, offs2, offs3, offs4, out,
+):
+    nc = tc.nc
+    with ExitStack() as ctx:
+        keep = ctx.enter_context(tc.tile_pool(name="keep", bufs=1))
+        psum = ctx.enter_context(tc.psum_pool(name="psum", bufs=1))
+
+        def sb(shape, dtype, name, tag=None, bufs=1):
+            return keep.tile(shape, dtype, name=name, tag=tag or name, bufs=bufs, align_bytes=ALIGN)
+
+        def bank(b, name):
+            return psum.tile([P, BANK], F32, name=name, tag=f"bank{b}")
+
+        def load_list(dram, entries, name):
+            tile = sb([P, entries // 16], U16, name)
+            nc.sync.dma_start(tile[:], dram)
+            return tile
+
+        def load_words(dram, a, width, name):
+            tile = sb([P, width], U32, name)
+            nc.sync.dma_start(
+                out=tile[:].bitcast(I32), in_=dram[a].rearrange("p t i -> p (t i)").bitcast(I32)
+            )
+            return tile
+
+        def load_planes(dram, first_row, name, queue):
+            passes, width = dram.shape[0], dram.shape[2]
+            tile = sb([P, width], U8, name)
+            nc.vector.memset(tile[:].bitcast(I32), 0)
+            for q in range(4):
+                rows = slice(32 * q + first_row, 32 * q + first_row + 4 * passes)
+                queue.dma_start(
+                    out=tile[rows, :].bitcast(I32), in_=dram[:, 4 * q : 4 * q + 4, :].bitcast(I32)
+                )
+            return tile
+
+        def load_w1(b):
+            raw = sb([P, PACK, BANK], F32, f"w1_raw{b}")
+            nc.sync.dma_start(
+                out=raw[:], in_=w1[:, b * BANK : (b + 1) * BANK].rearrange("(p j) c -> p j c", j=PACK)
+            )
+            return raw
+
+        def quantise_w1(b, raw):
+            rounded = sb([P, PACK * BANK], BF16, f"w1_bf{b}")
+            nc.scalar.copy(
+                out=rounded[:].rearrange("p (t m j) -> p m j t", t=PACK, j=PACK),
+                in_=raw[:].rearrange("p j (m t) -> p m j t", t=PACK),
+            )
+            codes = sb([P, BANK], U32, f"w1_codes{b}")
+            plane = sb([P, BANK], U8, f"w1_plane{b}")
+            nc.vector.quantize_mx(out=codes[:].bitcast(FP8X4), scales=plane[:], in_=rounded[:])
+            return codes, plane
+
+        page_rows = page0.rearrange("(b p t) c -> b t p c", b=2, t=PACK)
+
+        def load_page(s):
+            page = sb([P, T2], F32, f"page{s}", tag="page", bufs=4)
+            nc.sync.dma_start(out=page[:], in_=page_rows[s // PACK, s % PACK])
+            return page
+
+        def gather(table, lst, first, count, dtype, name, tag=None):
+            picked = sb([P, count], dtype, name, tag=tag)
+            nc.vector.tensor_copy(
+                picked[:], table[:].indirect(lst[:, first // 16 : (first + count) // 16])
+            )
+            return picked
+
+        idx = load_list(offs, S, "idx")
+        idx2 = load_list(offs2, S2, "idx2")
+        tab_planes = load_planes(tab_scales, TAB_PLANE_ROW[0], "tab_planes", nc.gpsimd)
+        w4_plane_raw = load_planes(w4_scales, 0, "w4_plane_raw", nc.gpsimd)
+
+        w4_raw = sb([P, 2 * H], U8, "w4_raw")
+        nc.sync.dma_start(out=w4_raw[:].bitcast(I32), in_=w4_words[0].bitcast(I32))
+        tab0 = load_words(tab_words, 0, T, "tab0")
+        w1_raw = [load_w1(0)]
+        tab1 = load_words(tab_words, 1, T, "tab1")
+        idx3 = load_list(offs3, S, "idx3")
+        gain_sb = sb([P, 2, PACK], F32, "gain_sb")
+        nc.sync.dma_start(out=gain_sb[:], in_=gain.rearrange("(b p t) -> p b t", b=2, t=PACK))
+        wgs_rows = wgs.rearrange("(q t) j -> q t j", t=PACK)
+        wgs_first = sb([P, S], F32, "wgs_first")
+        for q in range(4):
+            nc.sync.dma_start(out=wgs_first[32 * q : 32 * q + 32, :], in_=wgs_rows[:, 0, :])
+        pages = [load_page(0)]
+        idx4 = load_list(offs4, NB, "idx4")
+        season_sb = sb([P, 2, PACK], F32, "season_sb")
+        nc.sync.dma_start(out=season_sb[:], in_=season.rearrange("(b p t) -> p b t", b=2, t=PACK))
+        pages.append(load_page(1))
+        wgs_rest = sb([P, PACK - 1, S], F32, "wgs_rest")
+        for q in range(4):
+            nc.sync.dma_start(out=wgs_rest[32 * q : 32 * q + 32, :, :], in_=wgs_rows[:, 1:, :])
+        pages.append(load_page(2))
+        tab2_planes = load_planes(tab2_scales, TAB2_PLANE_ROW[0], "tab2_planes", nc.sync)
+        cand_sb = sb([P, M_TILES], F32, "cand_sb")
+        with nc.allow_non_contiguous_dma(reason="one offset for each output row"):
+            nc.sync.dma_start(out=cand_sb[:], in_=cand.rearrange("(i p) -> p i", p=P))
+        w1_raw.append(load_w1(1))
+        pages.append(load_page(3))
+        tab2 = [load_words(tab2_words, a, T3, f"tab2_{a}") for a in range(2)]
+
+        v_plane = gather(tab_planes, idx, 0, S, U8, "v_plane")
+        w4_codes = sb([P, 2 * H], U8, "w4_codes")
+        nc.vector.tensor_copy(
+            out=w4_codes[:].bitcast(U16).rearrange("p (b t q) -> p b t q", b=2, t=PACK),
+            in_=w4_raw[:].bitcast(U16).rearrange("p (b q t) -> p b t q", b=2, t=PACK),
+        )
+        w4_plane = sb([P, H], U8, "w4_plane")
+        nc.vector.tensor_copy(
+            out=w4_plane[:].rearrange("p (b t q) -> p b t q", b=2, t=PACK),
+            in_=w4_plane_raw[:].rearrange("p (b q t) -> p b t q", b=2, t=PACK),
+        )
+        v0 = gather(tab0, idx, 0, S, U32, "v0")
+        w1_q = [quantise_w1(0, w1_raw[0])]
+        v1 = [gather(tab1, idx, c * BANK, BANK, U32, f"v1_{c}") for c in range(2)]
+        v2_plane = gather(tab2_planes, idx2, 0, S2, U8, "v2_plane")
+
+        def first_product(s):
+            b, t = divmod(s, PACK)
+            h = sb([P, S], F32, f"h{s}", tag="h", bufs=3)
+            codes, plane = w1_q[b]
+            for c in range(2):
+                cols = slice(c * BANK, (c + 1) * BANK)
+                acc = bank((2 * s + c) % 8, f"h_acc{s}_{c}")
+                nc.tensor.matmul_mx(
+                    out=acc[:],
+                    lhsT=w4_codes[:, 2 * P * s : 2 * P * (s + 1)].bitcast(FP4X4),
+                    lhsT_scale=w4_plane[:, P * s : P * (s + 1)],
+                    rhs=v0[:, cols].bitcast(FP8X4),
+                    rhs_scale=v_plane[TAB_PLANE_ROW[0] :, cols],
+                    start=True,
+                    stop=False,
+                )
+                nc.tensor.matmul_mx(
+                    out=acc[:],
+                    lhsT=codes[:, P * t : P * (t + 1)].bitcast(FP8X4),
+                    lhsT_scale=plane[:, P * t : P * (t + 1)],
+                    rhs=v1[c][:].bitcast(FP8X4),
+                    rhs_scale=v_plane[TAB_PLANE_ROW[1] :, cols],
+                    start=False,
+                    stop=True,
+                )
+                nc.scalar.activation(
+                    out=h[:, cols], in_=acc[:], func=ACT.Copy, scale=gain_sb[:, b, t : t + 1]
+                )
+            return h
+
+        def scatter(s, h, pieces):
+            t = s % PACK
+            weights = wgs_first[:] if t == 0 else wgs_rest[:, t - 1, :]
+            width = S // pieces
+            for c in range(pieces):
+                cols = slice(c * width, (c + 1) * width)
+                nc.vector.tensor_tensor(
+                    pages[s][:].indirect(idx3[:, c * width // 16 : (c + 1) * width // 16]),
+                    h[:, cols],
+                    weights[:, cols],
+                    ALU.mult,
+                )
+
+        xa_bf = [sb([P, NB, PACK], BF16, f"xa_bf{b}") for b in range(2)]
+        xb_bf = [sb([P, NB, PACK], BF16, f"xb_bf{b}") for b in range(2)]
+
+        def view_beds(s):
+            b, t = divmod(s, PACK)
+            x = gather(pages[s], idx4, 0, NB, F32, f"x{s}", tag="x")
+            factor = season_sb[:, b, t : t + 1]
+            if s == SLICES - 1:
+                nc.vector.tensor_scalar(xb_bf[b][:, :, t], x[:], factor, None, ALU.mult)
+            else:
+                nc.scalar.activation(out=xb_bf[b][:, :, t], in_=x[:], func=ACT.Copy, scale=factor)
+            nc.scalar.activation(out=xa_bf[b][:, :, t], in_=x[:], func=ACT.Abs)
+
+        def quantise_x(rounded, codes, name):
+            plane = sb([P, NB], U8, name)
+            nc.vector.quantize_mx(
+                out=codes.bitcast(FP8X4), scales=plane[:], in_=rounded[:].rearrange("p n t -> p (n t)")
+            )
+            return codes, plane
+
+        v2 = {}
+
+        def second_pass(acc, i, b, moving):
+            half, col = divmod(i, HALF_TILES)
+            codes, plane = moving
+            nc.tensor.matmul_mx(
+                out=acc[:],
+                lhsT=v2[b, half][:, P * col : P * (col + 1)].bitcast(FP8X4),
+                lhsT_scale=v2_plane[TAB2_PLANE_ROW[b] :, P * i : P * (i + 1)],
+                rhs=codes.bitcast(FP8X4),
+                rhs_scale=plane[:],
+                start=(b == 0),
+                stop=(b == 1),
+            )
+
+        def squash(i, eb):
+            th = sb([P, NB], F32, f"tanh{i}", tag="tanh", bufs=4)
+            nc.scalar.activation(out=th[:], in_=eb[:], func=ACT.Tanh)
+            return th
+
+        def finish(i, ea, th):
+            prod = sb([P, NB], F32, f"prod{i}", tag="prod", bufs=3)
+            nc.vector.tensor_tensor(prod[:], ea[:], th[:], ALU.mult)
+            res = sb([P, NB], F32, f"res{i}", tag="res", bufs=4)
+            nc.gpsimd.tensor_scalar(res[:], prod[:], 1.0, cand_sb[:, i : i + 1], ALU.mult, ALU.add)
+            nc.sync.dma_start(out=out[P * i : P * (i + 1), :], in_=res[:])
+
+        for s in range(SLICES):
+            if s == PACK:
+                w1_q.append(quantise_w1(1, w1_raw[1]))
+                for b in range(2):
+                    v2[b, 0] = gather(tab2[b], idx2, 0, BANK, U32, f"v2_{b}_0")
+            if s >= len(pages):
+                pages.append(load_page(s))
+            h = first_product(s)
+            scatter(s, h, 2 if s == 0 else 1)
+            if s < SLICES - 1:
+                view_beds(s)
+
+        codes0 = sb([P, 2, NB], U32, "x_codes0", tag="wgs_rest")
+        xb_q = [quantise_x(xb_bf[0], codes0[:, 0, :], "xb_plane0")]
+        xa_q = [quantise_x(xa_bf[0], codes0[:, 1, :], "xa_plane0")]
+        eb = [bank(i, f"eb{i}") for i in range(HALF_TILES)]
+        ea = [bank(HALF_TILES + i, f"ea{i}") for i in range(HALF_TILES)]
+        for i in range(HALF_TILES):
+            second_pass(eb[i], i, 0, xb_q[0])
+        for i in range(HALF_TILES):
+            second_pass(ea[i], i, 0, xa_q[0])
+        view_beds(SLICES - 1)
+        xb_codes1 = sb([P, NB], U32, "xb_codes1")
+        xa_codes1 = sb([P, NB], U32, "xa_codes1")
+        xb_q.append(quantise_x(xb_bf[1], xb_codes1[:], "xb_plane1"))
+        xa_q.append(quantise_x(xa_bf[1], xa_codes1[:], "xa_plane1"))
+        v2[0, 1] = gather(tab2[0], idx2, BANK, BANK, U32, "v2_0_1", tag="x")
+        v2[1, 1] = gather(tab2[1], idx2, BANK, BANK, U32, "v2_1_1", tag="xa_bf1")
+        th = []
+        for i in range(HALF_TILES):
+            second_pass(eb[i], i, 1, xb_q[1])
+            th.append(squash(i, eb[i]))
+        for i in range(HALF_TILES):
+            second_pass(ea[i], i, 1, xa_q[1])
+            finish(i, ea[i], th[i])
+        for i in range(HALF_TILES, M_TILES):
+            acc = bank(i - HALF_TILES, f"eb{i}")
+            for b in range(2):
+                second_pass(acc, i, b, xb_q[b])
+            th.append(squash(i, acc))
+        for i in range(HALF_TILES, M_TILES):
+            acc = bank(i, f"ea{i}")
+            for b in range(2):
+                second_pass(acc, i, b, xa_q[b])
+            finish(i, acc, th[i])

@@ -54,13 +54,13 @@ def tile_list_seed_shop_candidates_kernel(
             )
             return tile
 
-        def load_planes(dram, first_row, name, queue):
+        def load_planes(dram, first_row, name):
             passes, width = dram.shape[0], dram.shape[2]
             tile = sb([P, width], U8, name)
             nc.vector.memset(tile[:].bitcast(I32), 0)
             for q in range(4):
                 rows = slice(32 * q + first_row, 32 * q + first_row + 4 * passes)
-                queue.dma_start(
+                nc.sync.dma_start(
                     out=tile[rows, :].bitcast(I32), in_=dram[:, 4 * q : 4 * q + 4, :].bitcast(I32)
                 )
             return tile
@@ -72,21 +72,23 @@ def tile_list_seed_shop_candidates_kernel(
             )
             return raw
 
-        def quantise_w1(b, raw):
-            rounded = sb([P, PACK * BANK], BF16, f"w1_bf{b}")
+        def quantise_w1(s):
+            b, t = divmod(s, PACK)
+            rounded = sb([P, P, PACK], BF16, f"w1_bf{s}", tag=f"w1_bf{t}")
             nc.scalar.copy(
-                out=rounded[:].rearrange("p (t m j) -> p m j t", t=PACK, j=PACK),
-                in_=raw[:].rearrange("p j (m t) -> p m j t", t=PACK),
+                out=rounded[:], in_=w1_raw[b][:].rearrange("p j (m t) -> p t m j", t=PACK)[:, t, :, :]
             )
-            codes = sb([P, BANK], U32, f"w1_codes{b}")
-            plane = sb([P, BANK], U8, f"w1_plane{b}")
-            nc.vector.quantize_mx(out=codes[:].bitcast(FP8X4), scales=plane[:], in_=rounded[:])
+            codes = sb([P, P], U32, f"w1_codes{s}")
+            plane = sb([P, P], U8, f"w1_plane{s}")
+            nc.vector.quantize_mx(
+                out=codes[:].bitcast(FP8X4), scales=plane[:], in_=rounded[:].rearrange("p m j -> p (m j)")
+            )
             return codes, plane
 
         page_rows = page0.rearrange("(b p t) c -> b t p c", b=2, t=PACK)
 
         def load_page(s):
-            page = sb([P, T2], F32, f"page{s}", tag="page", bufs=4)
+            page = sb([P, T2], F32, f"page{s}", tag="page", bufs=5)
             nc.sync.dma_start(out=page[:], in_=page_rows[s // PACK, s % PACK])
             return page
 
@@ -98,37 +100,37 @@ def tile_list_seed_shop_candidates_kernel(
             return picked
 
         idx = load_list(offs, S, "idx")
-        idx2 = load_list(offs2, S2, "idx2")
-        tab_planes = load_planes(tab_scales, TAB_PLANE_ROW[0], "tab_planes", nc.gpsimd)
-        w4_plane_raw = load_planes(w4_scales, 0, "w4_plane_raw", nc.gpsimd)
-
+        tab1 = load_words(tab_words, 1, T, "tab1")
+        tab_planes = load_planes(tab_scales, TAB_PLANE_ROW[0], "tab_planes")
         w4_raw = sb([P, 2 * H], U8, "w4_raw")
         nc.sync.dma_start(out=w4_raw[:].bitcast(I32), in_=w4_words[0].bitcast(I32))
-        tab0 = load_words(tab_words, 0, T, "tab0")
         w1_raw = [load_w1(0)]
-        tab1 = load_words(tab_words, 1, T, "tab1")
-        idx3 = load_list(offs3, S, "idx3")
+        idx2 = load_list(offs2, S2, "idx2")
+        tab2_planes = load_planes(tab2_scales, TAB2_PLANE_ROW[0], "tab2_planes")
+        tab0 = load_words(tab_words, 0, T, "tab0")
+        w4_plane_raw = load_planes(w4_scales, 0, "w4_plane_raw")
         gain_sb = sb([P, 2, PACK], F32, "gain_sb")
         nc.sync.dma_start(out=gain_sb[:], in_=gain.rearrange("(b p t) -> p b t", b=2, t=PACK))
+        idx3 = load_list(offs3, S, "idx3")
+        pages = [load_page(0)]
         wgs_rows = wgs.rearrange("(q t) j -> q t j", t=PACK)
         wgs_first = sb([P, S], F32, "wgs_first")
         for q in range(4):
             nc.sync.dma_start(out=wgs_first[32 * q : 32 * q + 32, :], in_=wgs_rows[:, 0, :])
-        pages = [load_page(0)]
-        idx4 = load_list(offs4, NB, "idx4")
-        season_sb = sb([P, 2, PACK], F32, "season_sb")
-        nc.sync.dma_start(out=season_sb[:], in_=season.rearrange("(b p t) -> p b t", b=2, t=PACK))
+        w1_raw.append(load_w1(1))
         pages.append(load_page(1))
         wgs_rest = sb([P, PACK - 1, S], F32, "wgs_rest")
         for q in range(4):
             nc.sync.dma_start(out=wgs_rest[32 * q : 32 * q + 32, :, :], in_=wgs_rows[:, 1:, :])
+        idx4 = load_list(offs4, NB, "idx4")
+        season_sb = sb([P, 2, PACK], F32, "season_sb")
+        nc.sync.dma_start(out=season_sb[:], in_=season.rearrange("(b p t) -> p b t", b=2, t=PACK))
         pages.append(load_page(2))
-        tab2_planes = load_planes(tab2_scales, TAB2_PLANE_ROW[0], "tab2_planes", nc.sync)
         cand_sb = sb([P, M_TILES], F32, "cand_sb")
         with nc.allow_non_contiguous_dma(reason="one offset for each output row"):
             nc.sync.dma_start(out=cand_sb[:], in_=cand.rearrange("(i p) -> p i", p=P))
-        w1_raw.append(load_w1(1))
         pages.append(load_page(3))
+        pages.append(load_page(4))
         tab2 = [load_words(tab2_words, a, T3, f"tab2_{a}") for a in range(2)]
 
         v_plane = gather(tab_planes, idx, 0, S, U8, "v_plane")
@@ -137,38 +139,46 @@ def tile_list_seed_shop_candidates_kernel(
             out=w4_codes[:].bitcast(U16).rearrange("p (b t q) -> p b t q", b=2, t=PACK),
             in_=w4_raw[:].bitcast(U16).rearrange("p (b q t) -> p b t q", b=2, t=PACK),
         )
-        w4_plane = sb([P, H], U8, "w4_plane")
-        nc.vector.tensor_copy(
-            out=w4_plane[:].rearrange("p (b t q) -> p b t q", b=2, t=PACK),
-            in_=w4_plane_raw[:].rearrange("p (b q t) -> p b t q", b=2, t=PACK),
-        )
-        v0 = gather(tab0, idx, 0, S, U32, "v0")
-        w1_q = [quantise_w1(0, w1_raw[0])]
-        v1 = [gather(tab1, idx, c * BANK, BANK, U32, f"v1_{c}") for c in range(2)]
+        v1 = gather(tab1, idx, 0, S, U32, "v1")
+        w1_q = [quantise_w1(s) for s in range(PACK)]
         v2_plane = gather(tab2_planes, idx2, 0, S2, U8, "v2_plane")
+        w4_plane_cols = w4_plane_raw[:].rearrange("p (b q t) -> p b t q", b=2, t=PACK)
+        w4_plane = []
+
+        def deal_w4_planes(first, count):
+            b, t = divmod(first, PACK)
+            dealt = sb([P, count, P], U8, f"w4_plane{first}")
+            nc.vector.tensor_copy(out=dealt[:], in_=w4_plane_cols[:, b, t : t + count, :])
+            w4_plane.extend(dealt[:, k, :] for k in range(count))
+
+        v0 = [gather(tab0, idx, 0, BANK, U32, "v0_0")]
+        deal_w4_planes(0, 1)
+        v0.append(gather(tab0, idx, BANK, BANK, U32, "v0_1"))
+        deal_w4_planes(1, PACK - 1)
+        deal_w4_planes(PACK, PACK)
 
         def first_product(s):
             b, t = divmod(s, PACK)
-            h = sb([P, S], F32, f"h{s}", tag="h", bufs=3)
-            codes, plane = w1_q[b]
+            h = sb([P, S], F32, f"h{s}", tag=f"h{s}")
+            codes, plane = w1_q[s]
             for c in range(2):
                 cols = slice(c * BANK, (c + 1) * BANK)
                 acc = bank((2 * s + c) % 8, f"h_acc{s}_{c}")
                 nc.tensor.matmul_mx(
                     out=acc[:],
-                    lhsT=w4_codes[:, 2 * P * s : 2 * P * (s + 1)].bitcast(FP4X4),
-                    lhsT_scale=w4_plane[:, P * s : P * (s + 1)],
-                    rhs=v0[:, cols].bitcast(FP8X4),
-                    rhs_scale=v_plane[TAB_PLANE_ROW[0] :, cols],
+                    lhsT=codes[:].bitcast(FP8X4),
+                    lhsT_scale=plane[:],
+                    rhs=v1[:, cols].bitcast(FP8X4),
+                    rhs_scale=v_plane[TAB_PLANE_ROW[1] :, cols],
                     start=True,
                     stop=False,
                 )
                 nc.tensor.matmul_mx(
                     out=acc[:],
-                    lhsT=codes[:, P * t : P * (t + 1)].bitcast(FP8X4),
-                    lhsT_scale=plane[:, P * t : P * (t + 1)],
-                    rhs=v1[c][:].bitcast(FP8X4),
-                    rhs_scale=v_plane[TAB_PLANE_ROW[1] :, cols],
+                    lhsT=w4_codes[:, 2 * P * s : 2 * P * (s + 1)].bitcast(FP4X4),
+                    lhsT_scale=w4_plane[s],
+                    rhs=v0[c][:].bitcast(FP8X4),
+                    rhs_scale=v_plane[TAB_PLANE_ROW[0] :, cols],
                     start=False,
                     stop=True,
                 )
@@ -195,7 +205,8 @@ def tile_list_seed_shop_candidates_kernel(
 
         def view_beds(s):
             b, t = divmod(s, PACK)
-            x = gather(pages[s], idx4, 0, NB, F32, f"x{s}", tag="x")
+            tag = f"h{s + 1}" if s < SLICES - 2 else "x"
+            x = gather(pages[s], idx4, 0, NB, F32, f"x{s}", tag=tag)
             factor = season_sb[:, b, t : t + 1]
             if s == SLICES - 1:
                 nc.vector.tensor_scalar(xb_bf[b][:, :, t], x[:], factor, None, ALU.mult)
@@ -226,7 +237,7 @@ def tile_list_seed_shop_candidates_kernel(
             )
 
         def squash(i, eb):
-            th = sb([P, NB], F32, f"tanh{i}", tag="tanh", bufs=4)
+            th = sb([P, NB], F32, f"tanh{i}", tag=f"h{i}")
             nc.scalar.activation(out=th[:], in_=eb[:], func=ACT.Tanh)
             return th
 
@@ -234,19 +245,25 @@ def tile_list_seed_shop_candidates_kernel(
             prod = sb([P, NB], F32, f"prod{i}", tag="prod", bufs=3)
             nc.vector.tensor_tensor(prod[:], ea[:], th[:], ALU.mult)
             res = sb([P, NB], F32, f"res{i}", tag="res", bufs=4)
-            nc.gpsimd.tensor_scalar(res[:], prod[:], 1.0, cand_sb[:, i : i + 1], ALU.mult, ALU.add)
+            offset = cand_sb[:, i : i + 1]
+            if i < HALF_TILES:
+                nc.vector.tensor_scalar(res[:], prod[:], offset, None, ALU.add)
+            else:
+                nc.scalar.activation(out=res[:], in_=prod[:], func=ACT.Identity, bias=offset)
             nc.sync.dma_start(out=out[P * i : P * (i + 1), :], in_=res[:])
 
         for s in range(SLICES):
             if s == PACK:
-                w1_q.append(quantise_w1(1, w1_raw[1]))
+                w1_q.extend(quantise_w1(s2) for s2 in range(PACK, SLICES))
                 for b in range(2):
                     v2[b, 0] = gather(tab2[b], idx2, 0, BANK, U32, f"v2_{b}_0")
             if s >= len(pages):
                 pages.append(load_page(s))
             h = first_product(s)
             scatter(s, h, 2 if s == 0 else 1)
-            if s < SLICES - 1:
+            if 0 < s < SLICES - 1:
+                view_beds(s - 1)
+            if s == SLICES - 2:
                 view_beds(s)
 
         codes0 = sb([P, 2, NB], U32, "x_codes0", tag="wgs_rest")
@@ -273,10 +290,11 @@ def tile_list_seed_shop_candidates_kernel(
             second_pass(ea[i], i, 1, xa_q[1])
             finish(i, ea[i], th[i])
         for i in range(HALF_TILES, M_TILES):
-            acc = bank(i - HALF_TILES, f"eb{i}")
-            for b in range(2):
-                second_pass(acc, i, b, xb_q[b])
-            th.append(squash(i, acc))
+            eb.append(bank(i - HALF_TILES, f"eb{i}"))
+            second_pass(eb[i], i, 0, xb_q[0])
+        for i in range(HALF_TILES, M_TILES):
+            second_pass(eb[i], i, 1, xb_q[1])
+            th.append(squash(i, eb[i]))
         for i in range(HALF_TILES, M_TILES):
             acc = bank(i, f"ea{i}")
             for b in range(2):

@@ -23,6 +23,7 @@ ALIGN = 64
 SLICES = H // P
 M_TILES = S2 // P
 HALF_TILES = M_TILES // 2
+QUADRANT_ORDER = (0, 2, 1, 3)
 TAB_PLANE_ROW = (0, 4)
 TAB2_PLANE_ROW = (8, 12)
 
@@ -54,13 +55,13 @@ def tile_list_seed_shop_candidates_kernel(
             )
             return tile
 
-        def load_planes(dram, first_row, name):
+        def load_planes(dram, first_row, name, queue):
             passes, width = dram.shape[0], dram.shape[2]
             tile = sb([P, width], U8, name)
             nc.vector.memset(tile[:].bitcast(I32), 0)
             for q in range(4):
                 rows = slice(32 * q + first_row, 32 * q + first_row + 4 * passes)
-                nc.sync.dma_start(
+                queue.dma_start(
                     out=tile[rows, :].bitcast(I32), in_=dram[:, 4 * q : 4 * q + 4, :].bitcast(I32)
                 )
             return tile
@@ -99,39 +100,42 @@ def tile_list_seed_shop_candidates_kernel(
             )
             return picked
 
+        def load_row_factors(dram, name):
+            tile = sb([P, 2, 2 * PACK], F32, name)
+            nc.sync.dma_start(
+                out=tile[:, :, :PACK], in_=dram.rearrange("(b p t) -> p b t", b=2, t=PACK)
+            )
+            return tile
+
+        tab_planes = load_planes(tab_scales, TAB_PLANE_ROW[0], "tab_planes", nc.gpsimd)
         idx = load_list(offs, S, "idx")
         tab1 = load_words(tab_words, 1, T, "tab1")
-        tab_planes = load_planes(tab_scales, TAB_PLANE_ROW[0], "tab_planes")
         w4_raw = sb([P, 2 * H], U8, "w4_raw")
         nc.sync.dma_start(out=w4_raw[:].bitcast(I32), in_=w4_words[0].bitcast(I32))
         w1_raw = [load_w1(0)]
-        idx2 = load_list(offs2, S2, "idx2")
-        tab2_planes = load_planes(tab2_scales, TAB2_PLANE_ROW[0], "tab2_planes")
         tab0 = load_words(tab_words, 0, T, "tab0")
-        w4_plane_raw = load_planes(w4_scales, 0, "w4_plane_raw")
-        gain_sb = sb([P, 2, PACK], F32, "gain_sb")
-        nc.sync.dma_start(out=gain_sb[:], in_=gain.rearrange("(b p t) -> p b t", b=2, t=PACK))
+        w4_plane_raw = load_planes(w4_scales, 0, "w4_plane_raw", nc.sync)
+        gain_sb = load_row_factors(gain, "gain_sb")
         idx3 = load_list(offs3, S, "idx3")
         pages = [load_page(0)]
         wgs_rows = wgs.rearrange("(q t) j -> q t j", t=PACK)
         wgs_first = sb([P, S], F32, "wgs_first")
-        for q in range(4):
+        for q in QUADRANT_ORDER:
             nc.sync.dma_start(out=wgs_first[32 * q : 32 * q + 32, :], in_=wgs_rows[:, 0, :])
         w1_raw.append(load_w1(1))
         pages.append(load_page(1))
         wgs_rest = sb([P, PACK - 1, S], F32, "wgs_rest")
-        for q in range(4):
+        for q in QUADRANT_ORDER:
             nc.sync.dma_start(out=wgs_rest[32 * q : 32 * q + 32, :, :], in_=wgs_rows[:, 1:, :])
         idx4 = load_list(offs4, NB, "idx4")
-        season_sb = sb([P, 2, PACK], F32, "season_sb")
-        nc.sync.dma_start(out=season_sb[:], in_=season.rearrange("(b p t) -> p b t", b=2, t=PACK))
-        pages.append(load_page(2))
+        season_sb = load_row_factors(season, "season_sb")
+        idx2 = load_list(offs2, S2, "idx2")
+        tab2_planes = load_planes(tab2_scales, TAB2_PLANE_ROW[0], "tab2_planes", nc.sync)
+        pages.extend(load_page(s) for s in range(2, 5))
+        tab2 = [load_words(tab2_words, a, T3, f"tab2_{a}") for a in range(2)]
         cand_sb = sb([P, M_TILES], F32, "cand_sb")
         with nc.allow_non_contiguous_dma(reason="one offset for each output row"):
             nc.sync.dma_start(out=cand_sb[:], in_=cand.rearrange("(i p) -> p i", p=P))
-        pages.append(load_page(3))
-        pages.append(load_page(4))
-        tab2 = [load_words(tab2_words, a, T3, f"tab2_{a}") for a in range(2)]
 
         v_plane = gather(tab_planes, idx, 0, S, U8, "v_plane")
         w4_codes = sb([P, 2 * H], U8, "w4_codes")
@@ -141,7 +145,6 @@ def tile_list_seed_shop_candidates_kernel(
         )
         v1 = gather(tab1, idx, 0, S, U32, "v1")
         w1_q = [quantise_w1(s) for s in range(PACK)]
-        v2_plane = gather(tab2_planes, idx2, 0, S2, U8, "v2_plane")
         w4_plane_cols = w4_plane_raw[:].rearrange("p (b q t) -> p b t q", b=2, t=PACK)
         w4_plane = []
 
@@ -200,19 +203,34 @@ def tile_list_seed_shop_candidates_kernel(
                     ALU.mult,
                 )
 
+        x, xb_rows = [], []
         xa_bf = [sb([P, NB, PACK], BF16, f"xa_bf{b}") for b in range(2)]
         xb_bf = [sb([P, NB, PACK], BF16, f"xb_bf{b}") for b in range(2)]
 
+        def woven(rows):
+            return rows[:].rearrange("p t (c i) -> p c t i", i=PACK)
+
+        def weave_target(tile):
+            return tile[:].rearrange("p (c i) t -> p c t i", i=PACK)
+
         def view_beds(s):
             b, t = divmod(s, PACK)
-            tag = f"h{s + 1}" if s < SLICES - 2 else "x"
-            x = gather(pages[s], idx4, 0, NB, F32, f"x{s}", tag=tag)
+            if t == 0:
+                x.append(sb([P, PACK, NB], F32, f"x{b}", tag="x"))
+                xb_rows.append(sb([P, PACK, NB], BF16, f"xb_rows{b}", tag="xb_rows"))
+            nc.vector.tensor_copy(x[b][:, t, :], pages[s][:].indirect(idx4[:]))
             factor = season_sb[:, b, t : t + 1]
             if s == SLICES - 1:
-                nc.vector.tensor_scalar(xb_bf[b][:, :, t], x[:], factor, None, ALU.mult)
+                nc.vector.tensor_scalar(xb_rows[b][:, t, :], x[b][:, t, :], factor, None, ALU.mult)
+                nc.vector.tensor_copy(out=weave_target(xb_bf[b]), in_=woven(xb_rows[b]))
             else:
-                nc.scalar.activation(out=xb_bf[b][:, :, t], in_=x[:], func=ACT.Copy, scale=factor)
-            nc.scalar.activation(out=xa_bf[b][:, :, t], in_=x[:], func=ACT.Abs)
+                nc.scalar.activation(
+                    out=xb_rows[b][:, t, :], in_=x[b][:, t, :], func=ACT.Copy, scale=factor
+                )
+            if t == PACK - 1:
+                nc.scalar.activation(out=weave_target(xa_bf[b]), in_=woven(x[b]), func=ACT.Abs)
+            if s == PACK - 1:
+                nc.scalar.copy(out=weave_target(xb_bf[b]), in_=woven(xb_rows[b]))
 
         def quantise_x(rounded, codes, name):
             plane = sb([P, NB], U8, name)
@@ -255,15 +273,14 @@ def tile_list_seed_shop_candidates_kernel(
         for s in range(SLICES):
             if s == PACK:
                 w1_q.extend(quantise_w1(s2) for s2 in range(PACK, SLICES))
+                v2_plane = gather(tab2_planes, idx2, 0, S2, U8, "v2_plane")
                 for b in range(2):
                     v2[b, 0] = gather(tab2[b], idx2, 0, BANK, U32, f"v2_{b}_0")
             if s >= len(pages):
                 pages.append(load_page(s))
             h = first_product(s)
             scatter(s, h, 2 if s == 0 else 1)
-            if 0 < s < SLICES - 1:
-                view_beds(s - 1)
-            if s == SLICES - 2:
+            if s < SLICES - 1:
                 view_beds(s)
 
         codes0 = sb([P, 2, NB], U32, "x_codes0", tag="wgs_rest")

@@ -100,38 +100,47 @@ def tile_list_seed_shop_candidates_kernel(
             )
             return picked
 
-        def load_row_factors(dram, name):
+        def load_row_factors(dram, name, queue):
             tile = sb([P, 2, 2 * PACK], F32, name)
-            nc.sync.dma_start(
+            queue.dma_start(
                 out=tile[:, :, :PACK], in_=dram.rearrange("(b p t) -> p b t", b=2, t=PACK)
             )
             return tile
 
+        wgs_rows = wgs.rearrange("(q t) j -> t q j", t=PACK)
+
+        def load_wgs(t, pieces):
+            tile = sb([P, S], F32, f"wgs{t}")
+            width = S // pieces
+            for first in range(0, S, width):
+                cols = slice(first, first + width)
+                for q in QUADRANT_ORDER:
+                    nc.sync.dma_start(out=tile[32 * q : 32 * q + 32, cols], in_=wgs_rows[t, :, cols])
+            return tile
+
+        gain_sb = load_row_factors(gain, "gain_sb", nc.gpsimd)
         tab_planes = load_planes(tab_scales, TAB_PLANE_ROW[0], "tab_planes", nc.gpsimd)
+        w4_plane_raw = load_planes(w4_scales, 0, "w4_plane_raw", nc.gpsimd)
         idx = load_list(offs, S, "idx")
         tab1 = load_words(tab_words, 1, T, "tab1")
         w4_raw = sb([P, 2 * H], U8, "w4_raw")
         nc.sync.dma_start(out=w4_raw[:].bitcast(I32), in_=w4_words[0].bitcast(I32))
         w1_raw = [load_w1(0)]
         tab0 = load_words(tab_words, 0, T, "tab0")
-        w4_plane_raw = load_planes(w4_scales, 0, "w4_plane_raw", nc.sync)
-        gain_sb = load_row_factors(gain, "gain_sb")
         idx3 = load_list(offs3, S, "idx3")
         pages = [load_page(0)]
-        wgs_rows = wgs.rearrange("(q t) j -> q t j", t=PACK)
-        wgs_first = sb([P, S], F32, "wgs_first")
-        for q in QUADRANT_ORDER:
-            nc.sync.dma_start(out=wgs_first[32 * q : 32 * q + 32, :], in_=wgs_rows[:, 0, :])
-        w1_raw.append(load_w1(1))
-        pages.append(load_page(1))
-        wgs_rest = sb([P, PACK - 1, S], F32, "wgs_rest")
-        for q in QUADRANT_ORDER:
-            nc.sync.dma_start(out=wgs_rest[32 * q : 32 * q + 32, :, :], in_=wgs_rows[:, 1:, :])
+        wgs_sb = [load_wgs(0, 2)]
         idx4 = load_list(offs4, NB, "idx4")
-        season_sb = load_row_factors(season, "season_sb")
+        pages.append(load_page(1))
+        wgs_sb.append(load_wgs(1, 1))
+        season_sb = load_row_factors(season, "season_sb", nc.sync)
+        w1_raw.append(load_w1(1))
+        for s in range(2, PACK):
+            pages.append(load_page(s))
+            wgs_sb.append(load_wgs(s, 1))
         idx2 = load_list(offs2, S2, "idx2")
         tab2_planes = load_planes(tab2_scales, TAB2_PLANE_ROW[0], "tab2_planes", nc.sync)
-        pages.extend(load_page(s) for s in range(2, 5))
+        pages.append(load_page(PACK))
         tab2 = [load_words(tab2_words, a, T3, f"tab2_{a}") for a in range(2)]
         cand_sb = sb([P, M_TILES], F32, "cand_sb")
         with nc.allow_non_contiguous_dma(reason="one offset for each output row"):
@@ -154,7 +163,7 @@ def tile_list_seed_shop_candidates_kernel(
             nc.vector.tensor_copy(out=dealt[:], in_=w4_plane_cols[:, b, t : t + count, :])
             w4_plane.extend(dealt[:, k, :] for k in range(count))
 
-        v0 = [gather(tab0, idx, 0, BANK, U32, "v0_0")]
+        v0 = [gather(tab0, idx, 0, BANK, U32, "v0_0", tag="tab_planes")]
         deal_w4_planes(0, 1)
         v0.append(gather(tab0, idx, BANK, BANK, U32, "v0_1"))
         deal_w4_planes(1, PACK - 1)
@@ -191,15 +200,13 @@ def tile_list_seed_shop_candidates_kernel(
             return h
 
         def scatter(s, h, pieces):
-            t = s % PACK
-            weights = wgs_first[:] if t == 0 else wgs_rest[:, t - 1, :]
             width = S // pieces
-            for c in range(pieces):
-                cols = slice(c * width, (c + 1) * width)
+            for first in range(0, S, width):
+                cols = slice(first, first + width)
                 nc.vector.tensor_tensor(
-                    pages[s][:].indirect(idx3[:, c * width // 16 : (c + 1) * width // 16]),
+                    pages[s][:].indirect(idx3[:, first // 16 : (first + width) // 16]),
                     h[:, cols],
-                    weights[:, cols],
+                    wgs_sb[s % PACK][:, cols],
                     ALU.mult,
                 )
 
@@ -260,12 +267,12 @@ def tile_list_seed_shop_candidates_kernel(
             return th
 
         def finish(i, ea, th):
-            prod = sb([P, NB], F32, f"prod{i}", tag="prod", bufs=3)
+            prod = sb([P, NB], F32, f"prod{i}", tag="prod", bufs=4)
             nc.vector.tensor_tensor(prod[:], ea[:], th[:], ALU.mult)
-            res = sb([P, NB], F32, f"res{i}", tag="res", bufs=4)
+            res = sb([P, NB], F32, f"res{i}", tag=f"h{i}")
             offset = cand_sb[:, i : i + 1]
             if i < HALF_TILES:
-                nc.vector.tensor_scalar(res[:], prod[:], offset, None, ALU.add)
+                nc.gpsimd.tensor_scalar(res[:], prod[:], 1.0, offset, ALU.mult, ALU.add)
             else:
                 nc.scalar.activation(out=res[:], in_=prod[:], func=ACT.Identity, bias=offset)
             nc.sync.dma_start(out=out[P * i : P * (i + 1), :], in_=res[:])
@@ -283,16 +290,16 @@ def tile_list_seed_shop_candidates_kernel(
             if s < SLICES - 1:
                 view_beds(s)
 
-        codes0 = sb([P, 2, NB], U32, "x_codes0", tag="wgs_rest")
+        codes0 = sb([P, 2, NB], U32, "x_codes0", tag=f"wgs{PACK - 1}")
         xb_q = [quantise_x(xb_bf[0], codes0[:, 0, :], "xb_plane0")]
-        xa_q = [quantise_x(xa_bf[0], codes0[:, 1, :], "xa_plane0")]
         eb = [bank(i, f"eb{i}") for i in range(HALF_TILES)]
         ea = [bank(HALF_TILES + i, f"ea{i}") for i in range(HALF_TILES)]
         for i in range(HALF_TILES):
             second_pass(eb[i], i, 0, xb_q[0])
+        view_beds(SLICES - 1)
+        xa_q = [quantise_x(xa_bf[0], codes0[:, 1, :], "xa_plane0")]
         for i in range(HALF_TILES):
             second_pass(ea[i], i, 0, xa_q[0])
-        view_beds(SLICES - 1)
         xb_codes1 = sb([P, NB], U32, "xb_codes1")
         xa_codes1 = sb([P, NB], U32, "xa_codes1")
         xb_q.append(quantise_x(xb_bf[1], xb_codes1[:], "xb_plane1"))

@@ -122,19 +122,19 @@ def tile_list_seed_shop_candidates_kernel(
         tab_planes = load_planes(tab_scales, TAB_PLANE_ROW[0], "tab_planes", nc.gpsimd)
         w4_plane_raw = load_planes(w4_scales, 0, "w4_plane_raw", nc.gpsimd)
         idx = load_list(offs, S, "idx")
-        tab1 = load_words(tab_words, 1, T, "tab1")
         w4_raw = sb([P, 2 * H], U8, "w4_raw")
         nc.sync.dma_start(out=w4_raw[:].bitcast(I32), in_=w4_words[0].bitcast(I32))
+        tab1 = load_words(tab_words, 1, T, "tab1")
         w1_raw = [load_w1(0)]
         tab0 = load_words(tab_words, 0, T, "tab0")
         idx3 = load_list(offs3, S, "idx3")
         pages = [load_page(0)]
         wgs_sb = [load_wgs(0, 2)]
         idx4 = load_list(offs4, NB, "idx4")
+        w1_raw.append(load_w1(1))
         pages.append(load_page(1))
         wgs_sb.append(load_wgs(1, 1))
         season_sb = load_row_factors(season, "season_sb", nc.sync)
-        w1_raw.append(load_w1(1))
         for s in range(2, PACK):
             pages.append(load_page(s))
             wgs_sb.append(load_wgs(s, 1))
@@ -268,14 +268,19 @@ def tile_list_seed_shop_candidates_kernel(
 
         def finish(i, ea, th):
             prod = sb([P, NB], F32, f"prod{i}", tag="prod", bufs=4)
-            nc.vector.tensor_tensor(prod[:], ea[:], th[:], ALU.mult)
             res = sb([P, NB], F32, f"res{i}", tag=f"h{i}")
             offset = cand_sb[:, i : i + 1]
-            if i < HALF_TILES:
-                nc.gpsimd.tensor_scalar(res[:], prod[:], 1.0, offset, ALU.mult, ALU.add)
-            else:
-                nc.scalar.activation(out=res[:], in_=prod[:], func=ACT.Identity, bias=offset)
-            nc.sync.dma_start(out=out[P * i : P * (i + 1), :], in_=res[:])
+            width = NB // 2 if i == M_TILES - 1 else NB
+            for first in range(0, NB, width):
+                cols = slice(first, first + width)
+                nc.vector.tensor_tensor(prod[:, cols], ea[:, cols], th[:, cols], ALU.mult)
+            for first in range(0, NB, width):
+                cols = slice(first, first + width)
+                if i < HALF_TILES:
+                    nc.gpsimd.tensor_scalar(res[:, cols], prod[:, cols], 1.0, offset, ALU.mult, ALU.add)
+                else:
+                    nc.scalar.activation(out=res[:, cols], in_=prod[:, cols], func=ACT.Identity, bias=offset)
+                nc.sync.dma_start(out=out[P * i : P * (i + 1), cols], in_=res[:, cols])
 
         for s in range(SLICES):
             if s == PACK:

from contextlib import ExitStack

import concourse.mybir as mybir

K, H, T, S, T3, S2, T2, NB = 1024, 1024, 4096, 1024, 2048, 1024, 2048, 512
FLOPS = 2 * K * H * S + 2 * 2 * H * S2 * NB

F32 = mybir.dt.float32
BF16 = mybir.dt.bfloat16
I32 = mybir.dt.int32
U32 = mybir.dt.uint32
U16 = mybir.dt.uint16
U8 = mybir.dt.uint8
FP8X4 = mybir.dt.float8_e4m3fn_x4
FP4X4 = mybir.dt.float4_e2m1fn_x4
ALU = mybir.AluOpType
ACT = mybir.ActivationFunctionType

P = 128
PACK = 4
BANK = 512
ALIGN = 64
SLICES = H // P
M_TILES = S2 // P
HALF_TILES = M_TILES // 2
QUADRANT_ORDER = (0, 2, 1, 3)
TAB_PLANE_ROW = (0, 4)
TAB2_PLANE_ROW = (8, 12)


def tile_list_seed_shop_candidates_kernel(
    tc, tab_words, tab_scales, tab2_words, tab2_scales, w4_words, w4_scales, w1, gain, page0, wgs,
    season, cand, offs, offs2, offs3, offs4, out,
):
    nc = tc.nc
    with ExitStack() as ctx:
        keep = ctx.enter_context(tc.tile_pool(name="keep", bufs=1))
        psum = ctx.enter_context(tc.psum_pool(name="psum", bufs=1))

        def sb(shape, dtype, name, tag=None, bufs=1):
            return keep.tile(shape, dtype, name=name, tag=tag or name, bufs=bufs, align_bytes=ALIGN)

        def bank(b, name):
            return psum.tile([P, BANK], F32, name=name, tag=f"bank{b}")

        def load_list(dram, entries, name):
            tile = sb([P, entries // 16], U16, name)
            nc.sync.dma_start(tile[:], dram)
            return tile

        def load_words(dram, a, width, name):
            tile = sb([P, width], U32, name)
            nc.sync.dma_start(
                out=tile[:].bitcast(I32), in_=dram[a].rearrange("p t i -> p (t i)").bitcast(I32)
            )
            return tile

        def load_planes(dram, first_row, name, queue):
            passes, width = dram.shape[0], dram.shape[2]
            tile = sb([P, width], U8, name)
            nc.vector.memset(tile[:].bitcast(I32), 0)
            for q in range(4):
                rows = slice(32 * q + first_row, 32 * q + first_row + 4 * passes)
                queue.dma_start(
                    out=tile[rows, :].bitcast(I32), in_=dram[:, 4 * q : 4 * q + 4, :].bitcast(I32)
                )
            return tile

        def load_w1(b):
            raw = sb([P, PACK, BANK], F32, f"w1_raw{b}")
            nc.sync.dma_start(
                out=raw[:], in_=w1[:, b * BANK : (b + 1) * BANK].rearrange("(p j) c -> p j c", j=PACK)
            )
            return raw

        def quantise_w1(s):
            b, t = divmod(s, PACK)
            rounded = sb([P, P, PACK], BF16, f"w1_bf{s}", tag=f"w1_bf{t}")
            nc.scalar.copy(
                out=rounded[:], in_=w1_raw[b][:].rearrange("p j (m t) -> p t m j", t=PACK)[:, t, :, :]
            )
            codes = sb([P, P], U32, f"w1_codes{s}")
            plane = sb([P, P], U8, f"w1_plane{s}")
            nc.vector.quantize_mx(
                out=codes[:].bitcast(FP8X4), scales=plane[:], in_=rounded[:].rearrange("p m j -> p (m j)")
            )
            return codes, plane

        page_rows = page0.rearrange("(b p t) c -> b t p c", b=2, t=PACK)

        def load_page(s):
            page = sb([P, T2], F32, f"page{s}", tag="page", bufs=5)
            nc.sync.dma_start(out=page[:], in_=page_rows[s // PACK, s % PACK])
            return page

        def gather(table, lst, first, count, dtype, name, tag=None):
            picked = sb([P, count], dtype, name, tag=tag)
            nc.vector.tensor_copy(
                picked[:], table[:].indirect(lst[:, first // 16 : (first + count) // 16])
            )
            return picked

        def load_row_factors(dram, name, queue):
            tile = sb([P, 2, 2 * PACK], F32, name)
            queue.dma_start(
                out=tile[:, :, :PACK], in_=dram.rearrange("(b p t) -> p b t", b=2, t=PACK)
            )
            return tile

        wgs_rows = wgs.rearrange("(q t) j -> t q j", t=PACK)

        def load_wgs(t, pieces):
            tile = sb([P, S], F32, f"wgs{t}")
            width = S // pieces
            for first in range(0, S, width):
                cols = slice(first, first + width)
                for q in QUADRANT_ORDER:
                    nc.sync.dma_start(out=tile[32 * q : 32 * q + 32, cols], in_=wgs_rows[t, :, cols])
            return tile

        gain_sb = load_row_factors(gain, "gain_sb", nc.gpsimd)
        tab_planes = load_planes(tab_scales, TAB_PLANE_ROW[0], "tab_planes", nc.gpsimd)
        w4_plane_raw = load_planes(w4_scales, 0, "w4_plane_raw", nc.gpsimd)
        idx = load_list(offs, S, "idx")
        w4_raw = sb([P, 2 * H], U8, "w4_raw")
        nc.sync.dma_start(out=w4_raw[:].bitcast(I32), in_=w4_words[0].bitcast(I32))
        tab1 = load_words(tab_words, 1, T, "tab1")
        w1_raw = [load_w1(0)]
        tab0 = load_words(tab_words, 0, T, "tab0")
        idx3 = load_list(offs3, S, "idx3")
        pages = [load_page(0)]
        wgs_sb = [load_wgs(0, 2)]
        idx4 = load_list(offs4, NB, "idx4")
        w1_raw.append(load_w1(1))
        pages.append(load_page(1))
        wgs_sb.append(load_wgs(1, 1))
        season_sb = load_row_factors(season, "season_sb", nc.sync)
        for s in range(2, PACK):
            pages.append(load_page(s))
            wgs_sb.append(load_wgs(s, 1))
        idx2 = load_list(offs2, S2, "idx2")
        tab2_planes = load_planes(tab2_scales, TAB2_PLANE_ROW[0], "tab2_planes", nc.sync)
        pages.append(load_page(PACK))
        tab2 = [load_words(tab2_words, a, T3, f"tab2_{a}") for a in range(2)]
        cand_sb = sb([P, M_TILES], F32, "cand_sb")
        with nc.allow_non_contiguous_dma(reason="one offset for each output row"):
            nc.sync.dma_start(out=cand_sb[:], in_=cand.rearrange("(i p) -> p i", p=P))

        v_plane = gather(tab_planes, idx, 0, S, U8, "v_plane")
        w4_codes = sb([P, 2 * H], U8, "w4_codes")
        nc.vector.tensor_copy(
            out=w4_codes[:].bitcast(U16).rearrange("p (b t q) -> p b t q", b=2, t=PACK),
            in_=w4_raw[:].bitcast(U16).rearrange("p (b q t) -> p b t q", b=2, t=PACK),
        )
        v1 = gather(tab1, idx, 0, S, U32, "v1")
        w1_q = [quantise_w1(s) for s in range(PACK)]
        w4_plane_cols = w4_plane_raw[:].rearrange("p (b q t) -> p b t q", b=2, t=PACK)
        w4_plane = []

        def deal_w4_planes(first, count):
            b, t = divmod(first, PACK)
            dealt = sb([P, count, P], U8, f"w4_plane{first}")
            nc.vector.tensor_copy(out=dealt[:], in_=w4_plane_cols[:, b, t : t + count, :])
            w4_plane.extend(dealt[:, k, :] for k in range(count))

        v0 = [gather(tab0, idx, 0, BANK, U32, "v0_0", tag="tab_planes")]
        deal_w4_planes(0, 1)
        v0.append(gather(tab0, idx, BANK, BANK, U32, "v0_1"))
        deal_w4_planes(1, PACK - 1)
        deal_w4_planes(PACK, PACK)

        def first_product(s):
            b, t = divmod(s, PACK)
            h = sb([P, S], F32, f"h{s}", tag=f"h{s}")
            codes, plane = w1_q[s]
            for c in range(2):
                cols = slice(c * BANK, (c + 1) * BANK)
                acc = bank((2 * s + c) % 8, f"h_acc{s}_{c}")
                nc.tensor.matmul_mx(
                    out=acc[:],
                    lhsT=codes[:].bitcast(FP8X4),
                    lhsT_scale=plane[:],
                    rhs=v1[:, cols].bitcast(FP8X4),
                    rhs_scale=v_plane[TAB_PLANE_ROW[1] :, cols],
                    start=True,
                    stop=False,
                )
                nc.tensor.matmul_mx(
                    out=acc[:],
                    lhsT=w4_codes[:, 2 * P * s : 2 * P * (s + 1)].bitcast(FP4X4),
                    lhsT_scale=w4_plane[s],
                    rhs=v0[c][:].bitcast(FP8X4),
                    rhs_scale=v_plane[TAB_PLANE_ROW[0] :, cols],
                    start=False,
                    stop=True,
                )
                nc.scalar.activation(
                    out=h[:, cols], in_=acc[:], func=ACT.Copy, scale=gain_sb[:, b, t : t + 1]
                )
            return h

        def scatter(s, h, pieces):
            width = S // pieces
            for first in range(0, S, width):
                cols = slice(first, first + width)
                nc.vector.tensor_tensor(
                    pages[s][:].indirect(idx3[:, first // 16 : (first + width) // 16]),
                    h[:, cols],
                    wgs_sb[s % PACK][:, cols],
                    ALU.mult,
                )

        x, xb_rows = [], []
        xa_bf = [sb([P, NB, PACK], BF16, f"xa_bf{b}") for b in range(2)]
        xb_bf = [sb([P, NB, PACK], BF16, f"xb_bf{b}") for b in range(2)]

        def woven(rows):
            return rows[:].rearrange("p t (c i) -> p c t i", i=PACK)

        def weave_target(tile):
            return tile[:].rearrange("p (c i) t -> p c t i", i=PACK)

        def view_beds(s):
            b, t = divmod(s, PACK)
            if t == 0:
                x.append(sb([P, PACK, NB], F32, f"x{b}", tag="x"))
                xb_rows.append(sb([P, PACK, NB], BF16, f"xb_rows{b}", tag="xb_rows"))
            nc.vector.tensor_copy(x[b][:, t, :], pages[s][:].indirect(idx4[:]))
            factor = season_sb[:, b, t : t + 1]
            if s == SLICES - 1:
                nc.vector.tensor_scalar(xb_rows[b][:, t, :], x[b][:, t, :], factor, None, ALU.mult)
                nc.vector.tensor_copy(out=weave_target(xb_bf[b]), in_=woven(xb_rows[b]))
            else:
                nc.scalar.activation(
                    out=xb_rows[b][:, t, :], in_=x[b][:, t, :], func=ACT.Copy, scale=factor
                )
            if t == PACK - 1:
                nc.scalar.activation(out=weave_target(xa_bf[b]), in_=woven(x[b]), func=ACT.Abs)
            if s == PACK - 1:
                nc.scalar.copy(out=weave_target(xb_bf[b]), in_=woven(xb_rows[b]))

        def quantise_x(rounded, codes, name):
            plane = sb([P, NB], U8, name)
            nc.vector.quantize_mx(
                out=codes.bitcast(FP8X4), scales=plane[:], in_=rounded[:].rearrange("p n t -> p (n t)")
            )
            return codes, plane

        v2 = {}

        def second_pass(acc, i, b, moving):
            half, col = divmod(i, HALF_TILES)
            codes, plane = moving
            nc.tensor.matmul_mx(
                out=acc[:],
                lhsT=v2[b, half][:, P * col : P * (col + 1)].bitcast(FP8X4),
                lhsT_scale=v2_plane[TAB2_PLANE_ROW[b] :, P * i : P * (i + 1)],
                rhs=codes.bitcast(FP8X4),
                rhs_scale=plane[:],
                start=(b == 0),
                stop=(b == 1),
            )

        def squash(i, eb):
            th = sb([P, NB], F32, f"tanh{i}", tag=f"h{i}")
            nc.scalar.activation(out=th[:], in_=eb[:], func=ACT.Tanh)
            return th

        def finish(i, ea, th):
            prod = sb([P, NB], F32, f"prod{i}", tag="prod", bufs=4)
            res = sb([P, NB], F32, f"res{i}", tag=f"h{i}")
            offset = cand_sb[:, i : i + 1]
            width = NB // 2 if i == M_TILES - 1 else NB
            for first in range(0, NB, width):
                cols = slice(first, first + width)
                nc.vector.tensor_tensor(prod[:, cols], ea[:, cols], th[:, cols], ALU.mult)
            for first in range(0, NB, width):
                cols = slice(first, first + width)
                if i < HALF_TILES:
                    nc.gpsimd.tensor_scalar(res[:, cols], prod[:, cols], 1.0, offset, ALU.mult, ALU.add)
                else:
                    nc.scalar.activation(out=res[:, cols], in_=prod[:, cols], func=ACT.Identity, bias=offset)
                nc.sync.dma_start(out=out[P * i : P * (i + 1), cols], in_=res[:, cols])

        for s in range(SLICES):
            if s == PACK:
                w1_q.extend(quantise_w1(s2) for s2 in range(PACK, SLICES))
                v2_plane = gather(tab2_planes, idx2, 0, S2, U8, "v2_plane")
                for b in range(2):
                    v2[b, 0] = gather(tab2[b], idx2, 0, BANK, U32, f"v2_{b}_0")
            if s >= len(pages):
                pages.append(load_page(s))
            h = first_product(s)
            scatter(s, h, 2 if s == 0 else 1)
            if s < SLICES - 1:
                view_beds(s)

        codes0 = sb([P, 2, NB], U32, "x_codes0", tag=f"wgs{PACK - 1}")
        xb_q = [quantise_x(xb_bf[0], codes0[:, 0, :], "xb_plane0")]
        eb = [bank(i, f"eb{i}") for i in range(HALF_TILES)]
        ea = [bank(HALF_TILES + i, f"ea{i}") for i in range(HALF_TILES)]
        for i in range(HALF_TILES):
            second_pass(eb[i], i, 0, xb_q[0])
        view_beds(SLICES - 1)
        xa_q = [quantise_x(xa_bf[0], codes0[:, 1, :], "xa_plane0")]
        for i in range(HALF_TILES):
            second_pass(ea[i], i, 0, xa_q[0])
        xb_codes1 = sb([P, NB], U32, "xb_codes1")
        xa_codes1 = sb([P, NB], U32, "xa_codes1")
        xb_q.append(quantise_x(xb_bf[1], xb_codes1[:], "xb_plane1"))
        xa_q.append(quantise_x(xa_bf[1], xa_codes1[:], "xa_plane1"))
        v2[0, 1] = gather(tab2[0], idx2, BANK, BANK, U32, "v2_0_1", tag="x")
        v2[1, 1] = gather(tab2[1], idx2, BANK, BANK, U32, "v2_1_1", tag="xa_bf1")
        th = []
        for i in range(HALF_TILES):
            second_pass(eb[i], i, 1, xb_q[1])
            th.append(squash(i, eb[i]))
        for i in range(HALF_TILES):
            second_pass(ea[i], i, 1, xa_q[1])
            finish(i, ea[i], th[i])
        for i in range(HALF_TILES, M_TILES):
            eb.append(bank(i - HALF_TILES, f"eb{i}"))
            second_pass(eb[i], i, 0, xb_q[0])
        for i in range(HALF_TILES, M_TILES):
            second_pass(eb[i], i, 1, xb_q[1])
            th.append(squash(i, eb[i]))
        for i in range(HALF_TILES, M_TILES):
            acc = bank(i, f"ea{i}")
            for b in range(2):
                second_pass(acc, i, b, xa_q[b])
            finish(i, acc, th[i])
